import numpy as np
import ml_dtypes


def mxq(x, axis, fmt="e4m3"):
    dtype, down = {"e4m3": (ml_dtypes.float8_e4m3fn, 7), "e5m2": (ml_dtypes.float8_e5m2, 14)}[fmt]
    v = np.moveaxis(np.asarray(x, np.float32).astype(ml_dtypes.bfloat16).astype(np.float64), axis, -1)
    blocks = v.reshape(v.shape[:-1] + (-1, 32))
    amax = np.abs(blocks).max(-1, keepdims=True)
    byte = np.maximum(np.where(amax > 0, np.frexp(amax)[1] - 1 + 127, 0) - down, 1)
    scale = np.exp2(byte - 127.0)
    codes = (blocks / scale).astype(np.float32).astype(dtype).astype(np.float64)
    return np.moveaxis((codes * scale).reshape(v.shape), -1, axis)


WIDE = False


def mx_kscale(k):
    if not WIDE:
        return np.ones(k)
    levels = np.array([10, -10, 5, -5, 0])
    if k % 512:
        return np.exp2(np.random.permutation(np.resize(levels, k // 32))).repeat(32)
    a = np.empty((k // 512, 16))
    for p in range(k // 512):
        a[p, :8] = np.random.permutation(np.resize(levels, 8))
        for g in range(8):
            far = levels[np.abs(levels - a[p, g]) >= 10]
            a[p, g + 8] = far[np.random.randint(len(far))]
    return np.exp2(a.ravel()).repeat(32)


BF16 = ml_dtypes.bfloat16


def bf(x):
    return np.asarray(x, np.float32).astype(BF16)


def f64(x):
    return np.asarray(x).astype(np.float64)

def planes(Y):
    n, m = Y.shape
    b = f64(bf(Y)).reshape(n // 32, 32, m)
    amax = np.abs(b).max(1)
    byte = np.clip(np.where(amax > 0, np.frexp(amax)[1] - 1 + 127 - 7, 1), 1, 254)
    codes = (b * np.exp2(127.0 - byte)[:, None, :]).reshape(n, m).astype(np.float32).astype(ml_dtypes.float8_e4m3fn).view(np.uint8)
    words = codes.reshape(n // 512, 128, 4, m).transpose(0, 1, 3, 2)
    return np.ascontiguousarray(words), np.ascontiguousarray(byte.astype(np.uint8).reshape(n // 512, 16, m))


N, P = 1024, 1024


def setup_inputs():
    s, t = mx_kscale(P), mx_kscale(N)
    x = np.random.standard_normal((N, P)) / s[None, :]
    g = np.random.standard_normal((N, P)) / np.sqrt(P) * s[None, :]
    c = (1.0 + 0.2 * np.random.standard_normal(N)) * t
    d = (1.0 + 0.2 * np.random.standard_normal(N)) / t
    eta = np.random.uniform(0.5, 0.8, N)
    return {"x": bf(x), "g": bf(g), "c": bf(c), "d": bf(d), "eta": bf(eta)}


def skew_gradient(x, g):
    s = mxq(g, 1, "e4m3") @ mxq(x.T, 0, "e4m3")
    return (s - s.T) / np.sqrt(2.0)


def core(x, g, c, d, eta):
    x, g, c, d, eta = f64(x), f64(g), f64(c), f64(d), f64(eta)
    n = x.shape[0]
    a = skew_gradient(x, g)
    l = a * c[None, :]
    r = d[:, None] * a
    q = (mxq(l, 1, "e4m3") @ mxq(r, 0, "e4m3")) / np.sqrt(n)
    step = eta[None, :]
    delta = -step * a + 0.5 * step * step * q
    return delta


def reference(x, g, c, d, eta):
    R_out = core(x, g, c, d, eta)
    words, scales = planes(R_out.T)
    return R_out, words, scales

@@ -1,0 +1,325 @@
+from contextlib import ExitStack
+import math
+
+import concourse.mybir as mybir
+from concourse.masks import make_identity
+
+F32 = mybir.dt.float32
+BF16 = mybir.dt.bfloat16
+I32 = mybir.dt.int32
+U32 = mybir.dt.uint32
+U8 = mybir.dt.uint8
+FP8X4 = mybir.dt.float8_e4m3fn_x4
+ALU = mybir.AluOpType
+COPY = mybir.ActivationFunctionType.Copy
+
+N = 1024
+P = 128
+FLOPS = 2 * 2 * N * N * N
+RSQRT2 = 1.0 / math.sqrt(2.0)
+
+
+def tile_skewgradientquadraticstep_kernel(tc, x, g, c, d, eta, out_0, out_1, out_2):
+    nc = tc.nc
+    with ExitStack() as ctx:
+        keep = ctx.enter_context(tc.tile_pool(name="keep", bufs=1))
+        xts = ctx.enter_context(tc.tile_pool(name="xts", bufs=4))
+        work = ctx.enter_context(tc.tile_pool(name="work", bufs=2))
+        psum = ctx.enter_context(tc.psum_pool(name="psum", bufs=8))
+        ctx.enter_context(tc.manual_schedule())
+
+        def new_bank():
+            return psum.tile([P, 512], F32, name="bank")
+
+        src = {"x": x.rearrange("(h m t) k -> h t m k", h=2, t=4), "g": g.rearrange("(h m t) k -> h t m k", h=2, t=4)}
+        raw = {}
+        for i in range(8):
+            for op in ("x", "g"):
+                raw[op, i] = keep.tile([P, N], BF16, name="raw_%s%d" % (op, i))
+                nc.sync.dma_start(out=raw[op, i][:], in_=src[op][i // 4, i % 4])
+
+        ident = keep.tile([P, P], F32, name="ident")
+        make_identity(nc, ident[:])
+
+        vecs = keep.tile([P, 512], BF16, name="vecs")
+        nc.vector.memset(vecs[:], 0.0)
+        for v, vec in enumerate((c, d, eta)):
+            nc.scalar.dma_start(out=vecs[2 * v : 2 * v + 2, :], in_=vec.rearrange("(h w) -> h w", h=2))
+
+        fac = {}
+
+        def make_factors():
+            words = vecs[:].bitcast(F32)
+            bank = new_bank()
+            for u in range(2):
+                nc.tensor.transpose(bank[:, 128 * u : 128 * u + 128], words[:, u : 256 : 2], ident[:])
+            fv = keep.tile([P, 6, 4], BF16, name="fv")
+            nc.vector.tensor_copy(
+                out=fv[:].rearrange("p r e -> p (r e)").bitcast(F32).rearrange("p (r u) -> p r u", u=2),
+                in_=bank[:, 0:256].rearrange("p (u r) -> p r u", u=2)[:, 0:6, :],
+            )
+            flat = fv[:].rearrange("p r e -> p (r e)")
+            for name, row, scale in (("l", 0, -RSQRT2), ("r", 8, RSQRT2), ("e", 16, RSQRT2)):
+                fac[name] = keep.tile([P, 8], F32, name="fac_" + name)
+                nc.vector.tensor_scalar(out=fac[name][:], in0=flat[:, row : row + 8], scalar1=scale, scalar2=None, op0=ALU.mult)
+            fac["h"] = keep.tile([P, 8], F32, name="fac_h")
+            nc.vector.scalar_tensor_tensor(
+                out=fac["h"][:], in0=flat[:, 16:24], scalar=1.0 / 64.0, in1=flat[:, 16:24], op0=ALU.mult, op1=ALU.mult
+            )
+
+        codes, scales, xt = {}, {}, {}
+
+        def transpose_in(op, i):
+            words = raw[op, i][:].bitcast(F32)
+            bank = new_bank()
+            for gi in range(2):
+                for u in range(2):
+                    lo = 128 * (2 * gi + u)
+                    nc.tensor.transpose(bank[:, lo : lo + 128], words[:, 256 * gi + u : 256 * gi + 256 : 2], ident[:])
+            t = xts.tile([P, 2, P, 4], BF16, name="xt_" + op, align_bytes=64)
+            xt[op, i] = t
+            nc.scalar.copy(
+                out=t[:].rearrange("p g m e -> p (g m e)").bitcast(F32).rearrange("p (g m u) -> p g m u", g=2, u=2),
+                in_=bank[:].rearrange("p (g u m) -> p g m u", g=2, u=2),
+            )
+
+        def quantize_in(op, i):
+            codes[op, i] = keep.tile([P, 2, P], U32, name="codes_%s%d" % (op, i), align_bytes=64)
+            scales[op, i] = keep.tile([P, 2, P], U8, name="scales_%s%d" % (op, i), align_bytes=64)
+            nc.vector.quantize_mx(
+                out=codes[op, i][:].rearrange("p g m -> p (g m)").bitcast(FP8X4),
+                scales=scales[op, i][:].rearrange("p g m -> p (g m)"),
+                in_=xt[op, i][:].rearrange("p g m e -> p (g m e)"),
+            )
+
+        def negate(i):
+            t = xts.tile([P, 2, P, 4], BF16, name="xt_n", align_bytes=64)
+            xt["n", i] = t
+            nc.vector.tensor_scalar(
+                out=t[:].rearrange("p g m e -> p (g m e)"), in0=xt["x", i][:].rearrange("p g m e -> p (g m e)"),
+                scalar1=-1.0, scalar2=None, op0=ALU.mult,
+            )
+
+        ea = keep.tile([P, 8, N], F32, name="ea")
+        abank, bf, qcodes, qscales = {}, {}, {}, {}
+
+        def mm1(h, s):
+            bank = new_bank()
+            abank[h, s] = bank
+            for t in range(4):
+                k = 4 * h + t
+                step = 0
+                for a, b in (("g", "x"), ("n", "g")):
+                    for gi in range(2):
+                        nc.tensor.matmul_mx(
+                            out=bank[:, 128 * t : 128 * t + 128],
+                            lhsT=codes[a, k][:, gi, :].bitcast(FP8X4),
+                            lhsT_scale=scales[a, k][:, gi, :],
+                            rhs=codes[b, s][:, gi, :].bitcast(FP8X4),
+                            rhs_scale=scales[b, s][:, gi, :],
+                            start=(step == 0),
+                            stop=(step == 3),
+                        )
+                        step += 1
+
+        def start_pair(h, s):
+            hp = s // 4
+            if ("r", h, hp) not in bf:
+                for o in ("r", "l"):
+                    bf[o, h, hp] = work.tile([P, 512, 4], BF16, name="bf_" + o, align_bytes=64)
+                    qcodes[o, h, hp] = keep.tile([P, 512], U32, name="qc_%s%d%d" % (o, h, hp), align_bytes=64)
+                    qscales[o, h, hp] = keep.tile([P, 512], U8, name="qs_%s%d%d" % (o, h, hp), align_bytes=64)
+
+        def r_out(h, s):
+            hp = s // 4
+            col = 128 * (s % 4)
+            nc.vector.tensor_tensor(
+                out=bf["r", h, hp][:, col : col + 128, :],
+                in0=abank[h, s][:].rearrange("p (t n) -> p n t", t=4),
+                in1=fac["r"][:, 4 * h : 4 * h + 4].unsqueeze(1).to_broadcast([P, 128, 4]),
+                op=ALU.mult,
+            )
+
+        def l_out(h, s):
+            col = 128 * (s % 4)
+            nc.vector.tensor_tensor(
+                out=bf["l", h, s // 4][:, col : col + 128, :],
+                in0=abank[h, s][:].rearrange("p (t n) -> p n t", t=4),
+                in1=fac["l"][:, 4 * h : 4 * h + 4].unsqueeze(1).to_broadcast([P, 128, 4]),
+                op=ALU.mult,
+            )
+
+        def e_out(h, s):
+            for t in range(4):
+                nc.scalar.activation(
+                    out=ea[:, 4 * h + t, 128 * s : 128 * s + 128],
+                    in_=abank[h, s][:, 128 * t : 128 * t + 128],
+                    func=COPY,
+                    scale=fac["e"][:, 4 * h + t : 4 * h + t + 1],
+                )
+
+        def quantize_pair(o, h, pair):
+            hp = pair // 2
+            col = 256 * (pair % 2)
+            nc.vector.quantize_mx(
+                out=qcodes[o, h, hp][:, col : col + 256].bitcast(FP8X4),
+                scales=qscales[o, h, hp][:, col : col + 256],
+                in_=bf[o, h, hp][:, col : col + 256, :].rearrange("p n t -> p (n t)"),
+            )
+
+        qbank, out_t, il, osb = {}, {}, {}, {}
+
+        def mm2(h, hp, t):
+            bank = new_bank()
+            qbank[h, hp, t] = bank
+            for k in range(2):
+                nc.tensor.matmul_mx(
+                    out=bank[:],
+                    lhsT=qcodes["r", k, h][:, 128 * t : 128 * t + 128].bitcast(FP8X4),
+                    lhsT_scale=qscales["r", k, h][:, 128 * t : 128 * t + 128],
+                    rhs=qcodes["l", k, hp][:].bitcast(FP8X4),
+                    rhs_scale=qscales["l", k, hp][:],
+                    start=(k == 0),
+                    stop=(k == 1),
+                )
+
+        def combine(h, hp, t):
+            if t == 0:
+                out_t[h, hp] = work.tile([P, 4, 512], F32, name="out_t", align_bytes=64)
+            nc.vector.scalar_tensor_tensor(
+                out=out_t[h, hp][:, t, :],
+                in0=qbank[h, hp, t][:],
+                scalar=fac["h"][:, 4 * h + t : 4 * h + t + 1],
+                in1=ea[:, 4 * h + t, 512 * hp : 512 * hp + 512],
+                op0=ALU.mult,
+                op1=ALU.add,
+            )
+
+        def interleave_out(h, hp, rows, engine):
+            if (h, hp) not in il:
+                il[h, hp] = work.tile([P, 2048], BF16, name="il", align_bytes=64)
+            out = il[h, hp][:].rearrange("p (m a t) -> p a m t", a=4, t=4)[:, :, rows, :]
+            in_ = out_t[h, hp][:].rearrange("p t (a m) -> p a m t", a=4)[:, :, rows, :]
+            if engine == "V":
+                nc.vector.tensor_copy(out=out, in_=in_)
+            else:
+                nc.scalar.copy(out=out, in_=in_)
+
+        def quantize_out(h, hp):
+            oc = keep.tile([P, 512], U32, name="oc_%d%d" % (h, hp), align_bytes=64)
+            osc = keep.tile([P, 512], U8, name="os_%d%d" % (h, hp), align_bytes=64)
+            nc.vector.quantize_mx(out=oc[:].bitcast(FP8X4), scales=osc[:], in_=il[h, hp][:])
+            cols = slice(512 * hp, 512 * hp + 512)
+            nc.sync.dma_start(
+                out=out_1[h, :, cols, :].rearrange("p m b -> p (m b)").bitcast(I32), in_=oc[:].bitcast(I32)
+            )
+            for quad in range(4):
+                nc.sync.dma_start(
+                    out=out_2[h, 4 * quad : 4 * quad + 4, cols].bitcast(I32),
+                    in_=osc[32 * quad : 32 * quad + 4, :].bitcast(I32),
+                )
+
+        out_rows = out_0.rearrange("(h m a) j -> h m a j", h=2, a=4)
+
+        obank = {}
+
+        def transpose_out(h, hp, a):
+            bank = new_bank()
+            obank[h, hp, a] = bank
+            for t in range(4):
+                nc.tensor.transpose(
+                    bank[:, 128 * t : 128 * t + 128], out_t[h, hp][:, t, 128 * a : 128 * a + 128], ident[:]
+                )
+
+        def copy_out(h, hp, a):
+            if a == 0:
+                osb[h, hp] = work.tile([P, 4, 512], F32, name="osb", align_bytes=64)
+            nc.scalar.copy(
+                out=osb[h, hp][:, a, :].rearrange("m (p t) -> m p t", t=4),
+                in_=obank[h, hp, a][:].rearrange("m (t p) -> m p t", t=4),
+            )
+            if a % 2 == 1:
+                nc.sync.dma_start(
+                    out=out_rows[hp, :, a - 1 : a + 1, 512 * h : 512 * h + 512], in_=osb[h, hp][:, a - 1 : a + 1, :]
+                )
+
+        banks = [(h, 4 * hp + t) for hp in range(2) for h in range(2) for t in range(4)]
+
+        def drain(bi):
+            h, s = banks[bi]
+            start_pair(h, s)
+            e_out(h, s)
+            r_out(h, s)
+            if bi % 2 == 0 and bi >= 2:
+                ph, ps = banks[bi - 2]
+                quantize_pair("r", ph, ps // 2)
+            l_out(h, s)
+            if bi % 2 == 0 and bi >= 2:
+                quantize_pair("l", ph, ps // 2)
+
+        for i in range(8):
+            transpose_in("x", i)
+            transpose_in("g", i)
+            quantize_in("x", i)
+            negate(i)
+            quantize_in("g", i)
+            quantize_in("n", i)
+            if i == 0:
+                make_factors()
+
+        first = (0, 0)
+        mm2_at = (11, 11, 12, 14)
+        combine_at = (10, 10, 11, 12)
+        lag = 3
+        for n in range(16 + lag):
+            if n < 16:
+                mm1(*banks[n])
+            if n >= lag:
+                drain(n - lag)
+            for t in range(4):
+                if mm2_at[t] == n:
+                    mm2(*first, t)
+            if n >= lag:
+                for t in range(4):
+                    if combine_at[t] == n - lag:
+                        combine(*first, t)
+            if n == 15:
+                for a in range(4):
+                    transpose_out(*first, a)
+            if n - lag == 14:
+                interleave_out(*first, slice(0, 128), "S")
+            if n - lag == 15:
+                quantize_out(*first)
+                for a in range(4):
+                    copy_out(*first, a)
+        ph, ps = banks[14]
+        quantize_pair("r", ph, ps // 2)
+        quantize_pair("l", ph, ps // 2)
+
+        def interleave_both(h, hp):
+            interleave_out(h, hp, slice(0, 80), "V")
+            interleave_out(h, hp, slice(80, 128), "S")
+
+        blocks = [(1, 0), (0, 1), (1, 1)]
+        for n, blk in enumerate(blocks):
+            prev = blocks[n - 1]
+            for t in range(4):
+                mm2(*blk, t)
+            if n > 0:
+                for a in range(4):
+                    transpose_out(*prev, a)
+            for t in range(4):
+                combine(*blk, t)
+                if n > 0:
+                    if t == 0:
+                        interleave_both(*prev)
+                    if t == 2:
+                        quantize_out(*prev)
+                    copy_out(*prev, t)
+        last = blocks[-1]
+        for a in range(4):
+            transpose_out(*last, a)
+        interleave_both(*last)
+        for a in range(4):
+            copy_out(*last, a)
+        quantize_out(*last)

@@ -33,8 +33,9 @@ def tile_skewgradientquadraticstep_kernel(tc, x, g, c, d, eta, out_0, out_1, out
 
         src = {"x": x.rearrange("(h m t) k -> h t m k", h=2, t=4), "g": g.rearrange("(h m t) k -> h t m k", h=2, t=4)}
         raw = {}
-        for i in range(8):
-            for op in ("x", "g"):
+        groups = [(0,), (1,), (2, 3), (4, 5), (6, 7)]
+        for op, i in [(op, i) for grp in groups for op in ("x", "g") for i in grp]:
+            if True:
                 raw[op, i] = keep.tile([P, N], BF16, name="raw_%s%d" % (op, i))
                 nc.sync.dma_start(out=raw[op, i][:], in_=src[op][i // 4, i % 4])
 
@@ -59,9 +60,10 @@ def tile_skewgradientquadraticstep_kernel(tc, x, g, c, d, eta, out_0, out_1, out
                 in_=bank[:, 0:256].rearrange("p (u r) -> p r u", u=2)[:, 0:6, :],
             )
             flat = fv[:].rearrange("p r e -> p (r e)")
-            for name, row, scale in (("l", 0, -RSQRT2), ("r", 8, RSQRT2), ("e", 16, RSQRT2)):
-                fac[name] = keep.tile([P, 8], F32, name="fac_" + name)
-                nc.vector.tensor_scalar(out=fac[name][:], in0=flat[:, row : row + 8], scalar1=scale, scalar2=None, op0=ALU.mult)
+            fac["rl"] = keep.tile([P, 2, 8], F32, name="fac_rl")
+            fac["e"] = keep.tile([P, 8], F32, name="fac_e")
+            for dst, row, scale in ((fac["rl"][:, 0, :], 8, RSQRT2), (fac["rl"][:, 1, :], 0, -RSQRT2), (fac["e"][:], 16, RSQRT2)):
+                nc.vector.tensor_scalar(out=dst, in0=flat[:, row : row + 8], scalar1=scale, scalar2=None, op0=ALU.mult)
             fac["h"] = keep.tile([P, 8], F32, name="fac_h")
             nc.vector.scalar_tensor_tensor(
                 out=fac["h"][:], in0=flat[:, 16:24], scalar=1.0 / 64.0, in1=flat[:, 16:24], op0=ALU.mult, op1=ALU.mult
@@ -69,36 +71,35 @@ def tile_skewgradientquadraticstep_kernel(tc, x, g, c, d, eta, out_0, out_1, out
 
         codes, scales, xt = {}, {}, {}
 
-        def transpose_in(op, i):
+        def transpose_in(op, grp, i):
             words = raw[op, i][:].bitcast(F32)
             bank = new_bank()
             for gi in range(2):
                 for u in range(2):
                     lo = 128 * (2 * gi + u)
                     nc.tensor.transpose(bank[:, lo : lo + 128], words[:, 256 * gi + u : 256 * gi + 256 : 2], ident[:])
-            t = xts.tile([P, 2, P, 4], BF16, name="xt_" + op, align_bytes=64)
-            xt[op, i] = t
+            if i == grp[0]:
+                xt[op, grp] = xts.tile([P, len(grp) * 1024], BF16, name="xt_" + op, align_bytes=64)
+            pos = i - grp[0]
             nc.scalar.copy(
-                out=t[:].rearrange("p g m e -> p (g m e)").bitcast(F32).rearrange("p (g m u) -> p g m u", g=2, u=2),
+                out=xt[op, grp][:, 1024 * pos : 1024 * pos + 1024].bitcast(F32).rearrange("p (g m u) -> p g m u", g=2, u=2),
                 in_=bank[:].rearrange("p (g u m) -> p g m u", g=2, u=2),
             )
 
-        def quantize_in(op, i):
-            codes[op, i] = keep.tile([P, 2, P], U32, name="codes_%s%d" % (op, i), align_bytes=64)
-            scales[op, i] = keep.tile([P, 2, P], U8, name="scales_%s%d" % (op, i), align_bytes=64)
-            nc.vector.quantize_mx(
-                out=codes[op, i][:].rearrange("p g m -> p (g m)").bitcast(FP8X4),
-                scales=scales[op, i][:].rearrange("p g m -> p (g m)"),
-                in_=xt[op, i][:].rearrange("p g m e -> p (g m e)"),
-            )
+        def quantize_in(op, grp):
+            width = 256 * len(grp)
+            c = keep.tile([P, width], U32, name="codes_%s%d" % (op, grp[0]), align_bytes=64)
+            s = keep.tile([P, width], U8, name="scales_%s%d" % (op, grp[0]), align_bytes=64)
+            nc.vector.quantize_mx(out=c[:].bitcast(FP8X4), scales=s[:], in_=xt[op, grp][:])
+            for i in grp:
+                for gi in range(2):
+                    lo = 256 * (i - grp[0]) + 128 * gi
+                    codes[op, i, gi] = c[:, lo : lo + 128].bitcast(FP8X4)
+                    scales[op, i, gi] = s[:, lo : lo + 128]
 
-        def negate(i):
-            t = xts.tile([P, 2, P, 4], BF16, name="xt_n", align_bytes=64)
-            xt["n", i] = t
-            nc.vector.tensor_scalar(
-                out=t[:].rearrange("p g m e -> p (g m e)"), in0=xt["x", i][:].rearrange("p g m e -> p (g m e)"),
-                scalar1=-1.0, scalar2=None, op0=ALU.mult,
-            )
+        def negate(grp):
+            xt["n", grp] = xts.tile([P, len(grp) * 1024], BF16, name="xt_n", align_bytes=64)
+            nc.vector.tensor_scalar(out=xt["n", grp][:], in0=xt["x", grp][:], scalar1=-1.0, scalar2=None, op0=ALU.mult)
 
         ea = keep.tile([P, 8, N], F32, name="ea")
         abank, bf, qcodes, qscales = {}, {}, {}, {}
@@ -113,40 +114,50 @@ def tile_skewgradientquadraticstep_kernel(tc, x, g, c, d, eta, out_0, out_1, out
                     for gi in range(2):
                         nc.tensor.matmul_mx(
                             out=bank[:, 128 * t : 128 * t + 128],
-                            lhsT=codes[a, k][:, gi, :].bitcast(FP8X4),
-                            lhsT_scale=scales[a, k][:, gi, :],
-                            rhs=codes[b, s][:, gi, :].bitcast(FP8X4),
-                            rhs_scale=scales[b, s][:, gi, :],
+                            lhsT=codes[a, k, gi],
+                            lhsT_scale=scales[a, k, gi],
+                            rhs=codes[b, s, gi],
+                            rhs_scale=scales[b, s, gi],
                             start=(step == 0),
                             stop=(step == 3),
                         )
                         step += 1
 
-        def start_pair(h, s):
-            hp = s // 4
-            if ("r", h, hp) not in bf:
-                for o in ("r", "l"):
-                    bf[o, h, hp] = work.tile([P, 512, 4], BF16, name="bf_" + o, align_bytes=64)
-                    qcodes[o, h, hp] = keep.tile([P, 512], U32, name="qc_%s%d%d" % (o, h, hp), align_bytes=64)
-                    qscales[o, h, hp] = keep.tile([P, 512], U8, name="qs_%s%d%d" % (o, h, hp), align_bytes=64)
+        scalar_l = {(0, 1), (1, 2), (0, 5), (0, 6), (0, 7), (1, 4), (1, 5), (1, 6)}
 
-        def r_out(h, s):
-            hp = s // 4
+        def start_quadrant(h, hp):
+            bf[h, hp] = work.tile([P, 2, 512, 4], BF16, name="bf_rl", align_bytes=64)
+            for o in ("r", "l"):
+                qcodes[o, h, hp] = keep.tile([P, 512], U32, name="qc_%s%d%d" % (o, h, hp), align_bytes=64)
+                qscales[o, h, hp] = keep.tile([P, 512], U8, name="qs_%s%d%d" % (o, h, hp), align_bytes=64)
+
+        def rl_out(h, s):
             col = 128 * (s % 4)
+            both = 1 if (h, s) in scalar_l else 2
             nc.vector.tensor_tensor(
-                out=bf["r", h, hp][:, col : col + 128, :],
-                in0=abank[h, s][:].rearrange("p (t n) -> p n t", t=4),
-                in1=fac["r"][:, 4 * h : 4 * h + 4].unsqueeze(1).to_broadcast([P, 128, 4]),
+                out=bf[h, s // 4][:, 0:both, col : col + 128, :],
+                in0=abank[h, s][:].rearrange("p (t n) -> p n t", t=4).unsqueeze(1).to_broadcast([P, both, 128, 4]),
+                in1=fac["rl"][:, 0:both, 4 * h : 4 * h + 4].unsqueeze(2).to_broadcast([P, both, 128, 4]),
                 op=ALU.mult,
             )
 
         def l_out(h, s):
             col = 128 * (s % 4)
-            nc.vector.tensor_tensor(
-                out=bf["l", h, s // 4][:, col : col + 128, :],
-                in0=abank[h, s][:].rearrange("p (t n) -> p n t", t=4),
-                in1=fac["l"][:, 4 * h : 4 * h + 4].unsqueeze(1).to_broadcast([P, 128, 4]),
-                op=ALU.mult,
+            st = work.tile([P, 4, 128], BF16, name="stage_l", align_bytes=64)
+            for t in range(4):
+                nc.scalar.activation(
+                    out=st[:, t, :],
+                    in_=abank[h, s][:, 128 * t : 128 * t + 128],
+                    func=COPY,
+                    scale=fac["rl"][:, 1, 4 * h + t : 4 * h + t + 1],
+                )
+            nc.gpsimd.tensor_scalar(
+                out=bf[h, s // 4][:, 1, col : col + 128, :],
+                in0=st[:].rearrange("p t n -> p n t"),
+                scalar1=1.0,
+                scalar2=0.0,
+                op0=ALU.mult,
+                op1=ALU.add,
             )
 
         def e_out(h, s):
@@ -164,7 +175,7 @@ def tile_skewgradientquadraticstep_kernel(tc, x, g, c, d, eta, out_0, out_1, out
             nc.vector.quantize_mx(
                 out=qcodes[o, h, hp][:, col : col + 256].bitcast(FP8X4),
                 scales=qscales[o, h, hp][:, col : col + 256],
-                in_=bf[o, h, hp][:, col : col + 256, :].rearrange("p n t -> p (n t)"),
+                in_=bf[h, hp][:, 0 if o == "r" else 1, col : col + 256, :].rearrange("p n t -> p (n t)"),
             )
 
         qbank, out_t, il, osb = {}, {}, {}, {}
@@ -238,67 +249,76 @@ def tile_skewgradientquadraticstep_kernel(tc, x, g, c, d, eta, out_0, out_1, out
                 out=osb[h, hp][:, a, :].rearrange("m (p t) -> m p t", t=4),
                 in_=obank[h, hp, a][:].rearrange("m (t p) -> m p t", t=4),
             )
-            if a % 2 == 1:
-                nc.sync.dma_start(
-                    out=out_rows[hp, :, a - 1 : a + 1, 512 * h : 512 * h + 512], in_=osb[h, hp][:, a - 1 : a + 1, :]
-                )
+            size = 1 if (h, hp) == (1, 1) else 2
+            if a % size == size - 1:
+                rows = slice(a + 1 - size, a + 1)
+                nc.sync.dma_start(out=out_rows[hp, :, rows, 512 * h : 512 * h + 512], in_=osb[h, hp][:, rows, :])
 
         banks = [(h, 4 * hp + t) for hp in range(2) for h in range(2) for t in range(4)]
 
         def drain(bi):
             h, s = banks[bi]
-            start_pair(h, s)
+            if s % 4 == 0:
+                start_quadrant(h, s // 4)
+            if bi == 15:
+                rl_out(h, s)
+            if (h, s) in scalar_l:
+                l_out(h, s)
             e_out(h, s)
-            r_out(h, s)
+            if bi != 15:
+                rl_out(h, s)
             if bi % 2 == 0 and bi >= 2:
-                ph, ps = banks[bi - 2]
-                quantize_pair("r", ph, ps // 2)
-            l_out(h, s)
-            if bi % 2 == 0 and bi >= 2:
-                quantize_pair("l", ph, ps // 2)
+                quantize_both(bi - 2)
 
-        for i in range(8):
-            transpose_in("x", i)
-            transpose_in("g", i)
-            quantize_in("x", i)
-            negate(i)
-            quantize_in("g", i)
-            quantize_in("n", i)
-            if i == 0:
+        def quantize_both(bi):
+            h, s = banks[bi]
+            quantize_pair("r", h, s // 2)
+            quantize_pair("l", h, s // 2)
+
+        for j, grp in enumerate(groups):
+            for op in ("x", "g"):
+                for i in grp:
+                    transpose_in(op, grp, i)
+            negate(grp)
+            quantize_in("x", grp)
+            quantize_in("n", grp)
+            quantize_in("g", grp)
+            if j == 0:
                 make_factors()
 
         first = (0, 0)
-        mm2_at = (11, 11, 12, 14)
-        combine_at = (10, 10, 11, 12)
+        mm2_at = (12, 12, 13, 14)
+        combine_at = (10, 10, 12, 13)
         lag = 3
         for n in range(16 + lag):
             if n < 16:
                 mm1(*banks[n])
+            if n - lag == 15:
+                interleave_out(*first, slice(0, 128), "S")
             if n >= lag:
                 drain(n - lag)
             for t in range(4):
                 if mm2_at[t] == n:
                     mm2(*first, t)
-            if n >= lag:
-                for t in range(4):
-                    if combine_at[t] == n - lag:
-                        combine(*first, t)
-            if n == 15:
+            for t in range(4):
+                if combine_at[t] == n - lag:
+                    combine(*first, t)
+            if n == 16:
                 for a in range(4):
                     transpose_out(*first, a)
-            if n - lag == 14:
-                interleave_out(*first, slice(0, 128), "S")
-            if n - lag == 15:
-                quantize_out(*first)
-                for a in range(4):
-                    copy_out(*first, a)
-        ph, ps = banks[14]
-        quantize_pair("r", ph, ps // 2)
-        quantize_pair("l", ph, ps // 2)
+        copy_out(*first, 0)
+        quantize_both(14)
+        quantize_out(*first)
+        for a in range(1, 4):
+            copy_out(*first, a)
+
+        vector_rows = {(1, 0): 64, (0, 1): 96, (1, 1): 128}
 
         def interleave_both(h, hp):
-            interleave_out(h, hp, slice(0, 80), "V")
-            interleave_out(h, hp, slice(80, 128), "S")
+            rows = vector_rows[h, hp]
+            interleave_out(h, hp, slice(0, rows), "V")
+            if rows < 128:
+                interleave_out(h, hp, slice(rows, 128), "S")
 
         blocks = [(1, 0), (0, 1), (1, 1)]
         for n, blk in enumerate(blocks):
@@ -313,13 +333,14 @@ def tile_skewgradientquadraticstep_kernel(tc, x, g, c, d, eta, out_0, out_1, out
                 if n > 0:
                     if t == 0:
                         interleave_both(*prev)
-                    if t == 2:
+                    if t == 3:
                         quantize_out(*prev)
                     copy_out(*prev, t)
         last = blocks[-1]
         for a in range(4):
             transpose_out(*last, a)
         interleave_both(*last)
-        for a in range(4):
+        for a in range(3):
             copy_out(*last, a)
         quantize_out(*last)
+        copy_out(*last, 3)

@@ -55,7 +55,7 @@ def tile_skewgradientquadraticstep_kernel(tc, x, g, c, d, eta, out_0, out_1, out
             for u in range(2):
                 nc.tensor.transpose(bank[:, 128 * u : 128 * u + 128], words[:, u : 256 : 2], ident[:])
             fv = keep.tile([P, 6, 4], BF16, name="fv")
-            nc.vector.tensor_copy(
+            nc.scalar.copy(
                 out=fv[:].rearrange("p r e -> p (r e)").bitcast(F32).rearrange("p (r u) -> p r u", u=2),
                 in_=bank[:, 0:256].rearrange("p (u r) -> p r u", u=2)[:, 0:6, :],
             )
@@ -63,7 +63,7 @@ def tile_skewgradientquadraticstep_kernel(tc, x, g, c, d, eta, out_0, out_1, out
             fac["rl"] = keep.tile([P, 2, 8], F32, name="fac_rl")
             fac["e"] = keep.tile([P, 8], F32, name="fac_e")
             for dst, row, scale in ((fac["rl"][:, 0, :], 8, RSQRT2), (fac["rl"][:, 1, :], 0, -RSQRT2), (fac["e"][:], 16, RSQRT2)):
-                nc.vector.tensor_scalar(out=dst, in0=flat[:, row : row + 8], scalar1=scale, scalar2=None, op0=ALU.mult)
+                nc.scalar.activation(out=dst, in_=flat[:, row : row + 8], func=COPY, scale=scale)
             fac["h"] = keep.tile([P, 8], F32, name="fac_h")
             nc.vector.scalar_tensor_tensor(
                 out=fac["h"][:], in0=flat[:, 16:24], scalar=1.0 / 64.0, in1=flat[:, 16:24], op0=ALU.mult, op1=ALU.mult
@@ -178,6 +178,13 @@ def tile_skewgradientquadraticstep_kernel(tc, x, g, c, d, eta, out_0, out_1, out
                 in_=bf[h, hp][:, 0 if o == "r" else 1, col : col + 256, :].rearrange("p n t -> p (n t)"),
             )
 
+        def quantize_quadrant(o, h, hp):
+            nc.vector.quantize_mx(
+                out=qcodes[o, h, hp][:].bitcast(FP8X4),
+                scales=qscales[o, h, hp][:],
+                in_=bf[h, hp][:, 0 if o == "r" else 1, :, :].rearrange("p n t -> p (n t)"),
+            )
+
         qbank, out_t, il, osb = {}, {}, {}, {}
 
         def mm2(h, hp, t):
@@ -272,6 +279,11 @@ def tile_skewgradientquadraticstep_kernel(tc, x, g, c, d, eta, out_0, out_1, out
 
         def quantize_both(bi):
             h, s = banks[bi]
+            if s < 4:
+                if s == 2:
+                    quantize_quadrant("r", h, 0)
+                    quantize_quadrant("l", h, 0)
+                return
             quantize_pair("r", h, s // 2)
             quantize_pair("l", h, s // 2)
 
@@ -279,11 +291,13 @@ def tile_skewgradientquadraticstep_kernel(tc, x, g, c, d, eta, out_0, out_1, out
             for op in ("x", "g"):
                 for i in grp:
                     transpose_in(op, grp, i)
+                if j == 4 and op == "x":
+                    mm1(*banks[0])
             negate(grp)
             quantize_in("x", grp)
             quantize_in("n", grp)
             quantize_in("g", grp)
-            if j == 0:
+            if j == 3:
                 make_factors()
 
         first = (0, 0)
@@ -291,7 +305,7 @@ def tile_skewgradientquadraticstep_kernel(tc, x, g, c, d, eta, out_0, out_1, out
         combine_at = (10, 10, 12, 13)
         lag = 3
         for n in range(16 + lag):
-            if n < 16:
+            if 0 < n < 16:
                 mm1(*banks[n])
             if n - lag == 15:
                 interleave_out(*first, slice(0, 128), "S")

from contextlib import ExitStack
import math

import concourse.mybir as mybir
from concourse.masks import make_identity

F32 = mybir.dt.float32
BF16 = mybir.dt.bfloat16
I32 = mybir.dt.int32
U32 = mybir.dt.uint32
U8 = mybir.dt.uint8
FP8X4 = mybir.dt.float8_e4m3fn_x4
ALU = mybir.AluOpType
COPY = mybir.ActivationFunctionType.Copy

N = 1024
P = 128
FLOPS = 2 * 2 * N * N * N
RSQRT2 = 1.0 / math.sqrt(2.0)


def tile_skewgradientquadraticstep_kernel(tc, x, g, c, d, eta, out_0, out_1, out_2):
    nc = tc.nc
    with ExitStack() as ctx:
        keep = ctx.enter_context(tc.tile_pool(name="keep", bufs=1))
        xts = ctx.enter_context(tc.tile_pool(name="xts", bufs=4))
        work = ctx.enter_context(tc.tile_pool(name="work", bufs=2))
        psum = ctx.enter_context(tc.psum_pool(name="psum", bufs=8))
        ctx.enter_context(tc.manual_schedule())

        def new_bank():
            return psum.tile([P, 512], F32, name="bank")

        src = {"x": x.rearrange("(h m t) k -> h t m k", h=2, t=4), "g": g.rearrange("(h m t) k -> h t m k", h=2, t=4)}
        raw = {}
        groups = [(0,), (1,), (2, 3), (4, 5), (6, 7)]
        for op, i in [(op, i) for grp in groups for op in ("x", "g") for i in grp]:
            if True:
                raw[op, i] = keep.tile([P, N], BF16, name="raw_%s%d" % (op, i))
                nc.sync.dma_start(out=raw[op, i][:], in_=src[op][i // 4, i % 4])

        ident = keep.tile([P, P], F32, name="ident")
        make_identity(nc, ident[:])

        vecs = keep.tile([P, 512], BF16, name="vecs")
        nc.vector.memset(vecs[:], 0.0)
        for v, vec in enumerate((c, d, eta)):
            nc.scalar.dma_start(out=vecs[2 * v : 2 * v + 2, :], in_=vec.rearrange("(h w) -> h w", h=2))

        fac = {}

        def make_factors():
            words = vecs[:].bitcast(F32)
            bank = new_bank()
            for u in range(2):
                nc.tensor.transpose(bank[:, 128 * u : 128 * u + 128], words[:, u : 256 : 2], ident[:])
            fv = keep.tile([P, 6, 4], BF16, name="fv")
            nc.scalar.copy(
                out=fv[:].rearrange("p r e -> p (r e)").bitcast(F32).rearrange("p (r u) -> p r u", u=2),
                in_=bank[:, 0:256].rearrange("p (u r) -> p r u", u=2)[:, 0:6, :],
            )
            flat = fv[:].rearrange("p r e -> p (r e)")
            fac["rl"] = keep.tile([P, 2, 8], F32, name="fac_rl")
            fac["e"] = keep.tile([P, 8], F32, name="fac_e")
            for dst, row, scale in ((fac["rl"][:, 0, :], 8, RSQRT2), (fac["rl"][:, 1, :], 0, -RSQRT2), (fac["e"][:], 16, RSQRT2)):
                nc.scalar.activation(out=dst, in_=flat[:, row : row + 8], func=COPY, scale=scale)
            fac["h"] = keep.tile([P, 8], F32, name="fac_h")
            nc.vector.scalar_tensor_tensor(
                out=fac["h"][:], in0=flat[:, 16:24], scalar=1.0 / 64.0, in1=flat[:, 16:24], op0=ALU.mult, op1=ALU.mult
            )

        codes, scales, xt = {}, {}, {}

        def transpose_in(op, grp, i):
            words = raw[op, i][:].bitcast(F32)
            bank = new_bank()
            for gi in range(2):
                for u in range(2):
                    lo = 128 * (2 * gi + u)
                    nc.tensor.transpose(bank[:, lo : lo + 128], words[:, 256 * gi + u : 256 * gi + 256 : 2], ident[:])
            if i == grp[0]:
                xt[op, grp] = xts.tile([P, len(grp) * 1024], BF16, name="xt_" + op, align_bytes=64)
            pos = i - grp[0]
            nc.scalar.copy(
                out=xt[op, grp][:, 1024 * pos : 1024 * pos + 1024].bitcast(F32).rearrange("p (g m u) -> p g m u", g=2, u=2),
                in_=bank[:].rearrange("p (g u m) -> p g m u", g=2, u=2),
            )

        def quantize_in(op, grp):
            width = 256 * len(grp)
            c = keep.tile([P, width], U32, name="codes_%s%d" % (op, grp[0]), align_bytes=64)
            s = keep.tile([P, width], U8, name="scales_%s%d" % (op, grp[0]), align_bytes=64)
            nc.vector.quantize_mx(out=c[:].bitcast(FP8X4), scales=s[:], in_=xt[op, grp][:])
            for i in grp:
                for gi in range(2):
                    lo = 256 * (i - grp[0]) + 128 * gi
                    codes[op, i, gi] = c[:, lo : lo + 128].bitcast(FP8X4)
                    scales[op, i, gi] = s[:, lo : lo + 128]

        def negate(grp):
            xt["n", grp] = xts.tile([P, len(grp) * 1024], BF16, name="xt_n", align_bytes=64)
            nc.vector.tensor_scalar(out=xt["n", grp][:], in0=xt["x", grp][:], scalar1=-1.0, scalar2=None, op0=ALU.mult)

        ea = keep.tile([P, 8, N], F32, name="ea")
        abank, bf, qcodes, qscales = {}, {}, {}, {}

        def mm1(h, s):
            bank = new_bank()
            abank[h, s] = bank
            for t in range(4):
                k = 4 * h + t
                step = 0
                for a, b in (("g", "x"), ("n", "g")):
                    for gi in range(2):
                        nc.tensor.matmul_mx(
                            out=bank[:, 128 * t : 128 * t + 128],
                            lhsT=codes[a, k, gi],
                            lhsT_scale=scales[a, k, gi],
                            rhs=codes[b, s, gi],
                            rhs_scale=scales[b, s, gi],
                            start=(step == 0),
                            stop=(step == 3),
                        )
                        step += 1

        scalar_l = {(0, 1), (1, 2), (0, 5), (0, 6), (0, 7), (1, 4), (1, 5), (1, 6)}

        def start_quadrant(h, hp):
            bf[h, hp] = work.tile([P, 2, 512, 4], BF16, name="bf_rl", align_bytes=64)
            for o in ("r", "l"):
                qcodes[o, h, hp] = keep.tile([P, 512], U32, name="qc_%s%d%d" % (o, h, hp), align_bytes=64)
                qscales[o, h, hp] = keep.tile([P, 512], U8, name="qs_%s%d%d" % (o, h, hp), align_bytes=64)

        def rl_out(h, s):
            col = 128 * (s % 4)
            both = 1 if (h, s) in scalar_l else 2
            nc.vector.tensor_tensor(
                out=bf[h, s // 4][:, 0:both, col : col + 128, :],
                in0=abank[h, s][:].rearrange("p (t n) -> p n t", t=4).unsqueeze(1).to_broadcast([P, both, 128, 4]),
                in1=fac["rl"][:, 0:both, 4 * h : 4 * h + 4].unsqueeze(2).to_broadcast([P, both, 128, 4]),
                op=ALU.mult,
            )

        def l_out(h, s):
            col = 128 * (s % 4)
            st = work.tile([P, 4, 128], BF16, name="stage_l", align_bytes=64)
            for t in range(4):
                nc.scalar.activation(
                    out=st[:, t, :],
                    in_=abank[h, s][:, 128 * t : 128 * t + 128],
                    func=COPY,
                    scale=fac["rl"][:, 1, 4 * h + t : 4 * h + t + 1],
                )
            nc.gpsimd.tensor_scalar(
                out=bf[h, s // 4][:, 1, col : col + 128, :],
                in0=st[:].rearrange("p t n -> p n t"),
                scalar1=1.0,
                scalar2=0.0,
                op0=ALU.mult,
                op1=ALU.add,
            )

        def e_out(h, s):
            for t in range(4):
                nc.scalar.activation(
                    out=ea[:, 4 * h + t, 128 * s : 128 * s + 128],
                    in_=abank[h, s][:, 128 * t : 128 * t + 128],
                    func=COPY,
                    scale=fac["e"][:, 4 * h + t : 4 * h + t + 1],
                )

        def quantize_pair(o, h, pair):
            hp = pair // 2
            col = 256 * (pair % 2)
            nc.vector.quantize_mx(
                out=qcodes[o, h, hp][:, col : col + 256].bitcast(FP8X4),
                scales=qscales[o, h, hp][:, col : col + 256],
                in_=bf[h, hp][:, 0 if o == "r" else 1, col : col + 256, :].rearrange("p n t -> p (n t)"),
            )

        def quantize_quadrant(o, h, hp):
            nc.vector.quantize_mx(
                out=qcodes[o, h, hp][:].bitcast(FP8X4),
                scales=qscales[o, h, hp][:],
                in_=bf[h, hp][:, 0 if o == "r" else 1, :, :].rearrange("p n t -> p (n t)"),
            )

        qbank, out_t, il, osb = {}, {}, {}, {}

        def mm2(h, hp, t):
            bank = new_bank()
            qbank[h, hp, t] = bank
            for k in range(2):
                nc.tensor.matmul_mx(
                    out=bank[:],
                    lhsT=qcodes["r", k, h][:, 128 * t : 128 * t + 128].bitcast(FP8X4),
                    lhsT_scale=qscales["r", k, h][:, 128 * t : 128 * t + 128],
                    rhs=qcodes["l", k, hp][:].bitcast(FP8X4),
                    rhs_scale=qscales["l", k, hp][:],
                    start=(k == 0),
                    stop=(k == 1),
                )

        def combine(h, hp, t):
            if t == 0:
                out_t[h, hp] = work.tile([P, 4, 512], F32, name="out_t", align_bytes=64)
            nc.vector.scalar_tensor_tensor(
                out=out_t[h, hp][:, t, :],
                in0=qbank[h, hp, t][:],
                scalar=fac["h"][:, 4 * h + t : 4 * h + t + 1],
                in1=ea[:, 4 * h + t, 512 * hp : 512 * hp + 512],
                op0=ALU.mult,
                op1=ALU.add,
            )

        def interleave_out(h, hp, rows, engine):
            if (h, hp) not in il:
                il[h, hp] = work.tile([P, 2048], BF16, name="il", align_bytes=64)
            out = il[h, hp][:].rearrange("p (m a t) -> p a m t", a=4, t=4)[:, :, rows, :]
            in_ = out_t[h, hp][:].rearrange("p t (a m) -> p a m t", a=4)[:, :, rows, :]
            if engine == "V":
                nc.vector.tensor_copy(out=out, in_=in_)
            else:
                nc.scalar.copy(out=out, in_=in_)

        def quantize_out(h, hp):
            oc = keep.tile([P, 512], U32, name="oc_%d%d" % (h, hp), align_bytes=64)
            osc = keep.tile([P, 512], U8, name="os_%d%d" % (h, hp), align_bytes=64)
            nc.vector.quantize_mx(out=oc[:].bitcast(FP8X4), scales=osc[:], in_=il[h, hp][:])
            cols = slice(512 * hp, 512 * hp + 512)
            nc.sync.dma_start(
                out=out_1[h, :, cols, :].rearrange("p m b -> p (m b)").bitcast(I32), in_=oc[:].bitcast(I32)
            )
            for quad in range(4):
                nc.sync.dma_start(
                    out=out_2[h, 4 * quad : 4 * quad + 4, cols].bitcast(I32),
                    in_=osc[32 * quad : 32 * quad + 4, :].bitcast(I32),
                )

        out_rows = out_0.rearrange("(h m a) j -> h m a j", h=2, a=4)

        obank = {}

        def transpose_out(h, hp, a):
            bank = new_bank()
            obank[h, hp, a] = bank
            for t in range(4):
                nc.tensor.transpose(
                    bank[:, 128 * t : 128 * t + 128], out_t[h, hp][:, t, 128 * a : 128 * a + 128], ident[:]
                )

        def copy_out(h, hp, a):
            if a == 0:
                osb[h, hp] = work.tile([P, 4, 512], F32, name="osb", align_bytes=64)
            nc.scalar.copy(
                out=osb[h, hp][:, a, :].rearrange("m (p t) -> m p t", t=4),
                in_=obank[h, hp, a][:].rearrange("m (t p) -> m p t", t=4),
            )
            size = 1 if (h, hp) == (1, 1) else 2
            if a % size == size - 1:
                rows = slice(a + 1 - size, a + 1)
                nc.sync.dma_start(out=out_rows[hp, :, rows, 512 * h : 512 * h + 512], in_=osb[h, hp][:, rows, :])

        banks = [(h, 4 * hp + t) for hp in range(2) for h in range(2) for t in range(4)]

        def drain(bi):
            h, s = banks[bi]
            if s % 4 == 0:
                start_quadrant(h, s // 4)
            if bi == 15:
                rl_out(h, s)
            if (h, s) in scalar_l:
                l_out(h, s)
            e_out(h, s)
            if bi != 15:
                rl_out(h, s)
            if bi % 2 == 0 and bi >= 2:
                quantize_both(bi - 2)

        def quantize_both(bi):
            h, s = banks[bi]
            if s < 4:
                if s == 2:
                    quantize_quadrant("r", h, 0)
                    quantize_quadrant("l", h, 0)
                return
            quantize_pair("r", h, s // 2)
            quantize_pair("l", h, s // 2)

        for j, grp in enumerate(groups):
            for op in ("x", "g"):
                for i in grp:
                    transpose_in(op, grp, i)
                if j == 4 and op == "x":
                    mm1(*banks[0])
            negate(grp)
            quantize_in("x", grp)
            quantize_in("n", grp)
            quantize_in("g", grp)
            if j == 3:
                make_factors()

        first = (0, 0)
        mm2_at = (12, 12, 13, 14)
        combine_at = (10, 10, 12, 13)
        lag = 3
        for n in range(16 + lag):
            if 0 < n < 16:
                mm1(*banks[n])
            if n - lag == 15:
                interleave_out(*first, slice(0, 128), "S")
            if n >= lag:
                drain(n - lag)
            for t in range(4):
                if mm2_at[t] == n:
                    mm2(*first, t)
            for t in range(4):
                if combine_at[t] == n - lag:
                    combine(*first, t)
            if n == 16:
                for a in range(4):
                    transpose_out(*first, a)
        copy_out(*first, 0)
        quantize_both(14)
        quantize_out(*first)
        for a in range(1, 4):
            copy_out(*first, a)

        vector_rows = {(1, 0): 64, (0, 1): 96, (1, 1): 128}

        def interleave_both(h, hp):
            rows = vector_rows[h, hp]
            interleave_out(h, hp, slice(0, rows), "V")
            if rows < 128:
                interleave_out(h, hp, slice(rows, 128), "S")

        blocks = [(1, 0), (0, 1), (1, 1)]
        for n, blk in enumerate(blocks):
            prev = blocks[n - 1]
            for t in range(4):
                mm2(*blk, t)
            if n > 0:
                for a in range(4):
                    transpose_out(*prev, a)
            for t in range(4):
                combine(*blk, t)
                if n > 0:
                    if t == 0:
                        interleave_both(*prev)
                    if t == 3:
                        quantize_out(*prev)
                    copy_out(*prev, t)
        last = blocks[-1]
        for a in range(4):
            transpose_out(*last, a)
        interleave_both(*last)
        for a in range(3):
            copy_out(*last, a)
        quantize_out(*last)
        copy_out(*last, 3)
